import numpy as np
import ml_dtypes


def mxq(x, axis, fmt="e4m3"):
    dtype, down = {"e4m3": (ml_dtypes.float8_e4m3fn, 7), "e5m2": (ml_dtypes.float8_e5m2, 14)}[fmt]
    v = np.moveaxis(np.asarray(x, np.float32).astype(ml_dtypes.bfloat16).astype(np.float64), axis, -1)
    blocks = v.reshape(v.shape[:-1] + (-1, 32))
    amax = np.abs(blocks).max(-1, keepdims=True)
    byte = np.maximum(np.where(amax > 0, np.frexp(amax)[1] - 1 + 127, 0) - down, 1)
    scale = np.exp2(byte - 127.0)
    codes = (blocks / scale).astype(np.float32).astype(dtype).astype(np.float64)
    return np.moveaxis((codes * scale).reshape(v.shape), -1, axis)


WIDE = False


def mx_kscale(k):
    if not WIDE:
        return np.ones(k)
    levels = np.array([10, -10, 5, -5, 0])
    if k % 512:
        return np.exp2(np.random.permutation(np.resize(levels, k // 32))).repeat(32)
    a = np.empty((k // 512, 16))
    for p in range(k // 512):
        a[p, :8] = np.random.permutation(np.resize(levels, 8))
        for g in range(8):
            far = levels[np.abs(levels - a[p, g]) >= 10]
            a[p, g + 8] = far[np.random.randint(len(far))]
    return np.exp2(a.ravel()).repeat(32)


def f64(x):
    return np.asarray(x).astype(np.float64)


def striped(idx):
    return np.tile(np.asarray(idx).reshape(-1, 16).T, (8, 1)).astype(np.uint16)


def unstriped(offs):
    return offs[:16].T.reshape(-1).astype(np.int64)


def striped8(idx):
    return np.asarray(idx).reshape(8, -1, 16).transpose(0, 2, 1).reshape(128, -1).astype(np.uint16)


def unstriped8(offs):
    return offs.reshape(8, 16, -1).transpose(0, 2, 1).reshape(8, -1).astype(np.int64)


def pick8(x, idx, run):
    r = np.arange(len(x))
    return x[r[:, None], idx[r % (8 * run) // run]]


E2M1 = np.array([0.0, 0.5, 1.0, 1.5, 2.0, 3.0, 4.0, 6.0, -0.0, -0.5, -1.0, -1.5, -2.0, -3.0, -4.0, -6.0])


def pack_weight(w, fmt):
    k, n = w.shape
    w = f64(np.asarray(w, np.float32).astype(ml_dtypes.bfloat16)).reshape(k // 32, 32, n)
    amax = np.abs(w).max(1)
    if fmt == "e4m3":
        byte = np.frexp(amax)[1] - 1 + 127 - 7
    else:
        mant, ex = np.frexp(amax / 6.0)
        byte = np.where(mant > 0.5, ex, ex - 1) + 127
    byte = np.clip(np.where(amax > 0, byte, 1), 1, 254)
    scaled = (w * np.exp2(127.0 - byte)[:, None, :]).reshape(k, n).astype(np.float32)
    by_word = np.ascontiguousarray(scaled.reshape(k // 512, 128, 4, n).transpose(0, 1, 3, 2))
    if fmt == "e4m3":
        words = by_word.astype(ml_dtypes.float8_e4m3fn).view(np.uint8)
    else:
        c = by_word.astype(ml_dtypes.float4_e2m1fn).view(np.uint8) & 0xF
        words = (c[..., 0::2] | (c[..., 1::2] << 4)).reshape(k // 512, 128, 2 * n)
    return np.ascontiguousarray(words), np.ascontiguousarray(byte.astype(np.uint8).reshape(k // 512, 16, n))


def unpack_weight(words, scales, fmt):
    g, _, n = scales.shape
    words = np.ascontiguousarray(words).reshape(g, 128, n, -1)
    if fmt == "e4m3":
        vals = words.view(ml_dtypes.float8_e4m3fn).astype(np.float64)
    else:
        nib = np.empty((g, 128, n, 4), np.uint8)
        nib[..., 0::2] = words & 0xF
        nib[..., 1::2] = words >> 4
        vals = E2M1[nib]
    vals = vals * np.repeat(np.exp2(scales.astype(np.float64) - 127.0), 8, axis=1)[..., None]
    return vals.transpose(0, 1, 3, 2).reshape(g * 512, n)


K, J, R, T, Z, M, O, S, C, N = 512, 512, 512, 2048, 512, 1024, 256, 256, 512, 256


def setup_inputs():
    n = np.random.standard_normal
    idx = np.random.permutation(T)[:J]
    idx2 = np.random.permutation(M)[:J]
    idx3 = np.stack([np.random.permutation(J)[:S] for _ in range(8)])
    idx4 = np.stack([np.random.permutation(C)[:S] for _ in range(8)])
    idx5 = np.stack([np.random.permutation(C)[:S] for _ in range(8)])
    idx6 = np.stack([np.random.permutation(C)[:S] for _ in range(8)])
    idx7 = np.stack([np.random.permutation(C)[:O] for _ in range(8)])
    fk = mx_kscale(K)
    fr = mx_kscale(R)
    fz = mx_kscale(Z)
    xtp = pack_weight(n((K, T)) * fk[:, None], "e2m1")
    wp = pack_weight(n((K, R)) * 1 / np.sqrt(K) / fk[:, None] * fr, "e4m3")
    xop = pack_weight(n((Z, M)) / fz[:, None], "e2m1")
    w2p = pack_weight(n((Z, R)) * 1 / np.sqrt(Z) * fz[:, None] * fr, "e4m3")
    wbp = pack_weight(n((R, N)) * 1 / np.sqrt(R) / fr[:, None], "e4m3")
    return {
        "xt_words": xtp[0],
        "xt_scales": xtp[1],
        "w_words": wp[0],
        "w_scales": wp[1],
        "xo_words": xop[0],
        "xo_scales": xop[1],
        "w2_words": w2p[0],
        "w2_scales": w2p[1],
        "sa": (np.random.uniform(0.5, 1.6, (R, 1))).astype(np.float32),
        "sb": (np.random.uniform(0.5, 1.6, (R, 1))).astype(np.float32),
        "wb_words": wbp[0],
        "wb_scales": wbp[1],
        "offs": striped(idx),
        "offs2": striped(idx2),
        "offs3": striped8(idx3),
        "offs4": striped8(idx4),
        "offs5": striped8(idx5),
        "offs6": striped8(idx6),
        "offs7": striped8(idx7),
    }


def reference(xt_words, xt_scales, w_words, w_scales, xo_words, xo_scales, w2_words, w2_scales, sa, sb, wb_words, wb_scales, offs, offs2, offs3, offs4, offs5, offs6, offs7):
    idx = unstriped(offs)
    idx2 = unstriped(offs2)
    idx3 = unstriped8(offs3)
    idx4 = unstriped8(offs4)
    idx5 = unstriped8(offs5)
    idx6 = unstriped8(offs6)
    idx7 = unstriped8(offs7)
    xtu = unpack_weight(xt_words, xt_scales, "e2m1")
    wu = unpack_weight(w_words, w_scales, "e4m3")
    xou = unpack_weight(xo_words, xo_scales, "e2m1")
    w2u = unpack_weight(w2_words, w2_scales, "e4m3")
    wbu = unpack_weight(wb_words, wb_scales, "e4m3")
    xtidxg = xtu[:, idx]
    xoidx2g = xou[:, idx2]
    a = wu.T @ xtidxg + w2u.T @ xoidx2g
    h1 = pick8(a, idx3, 64) * f64(sa)
    pw = np.zeros((R, C))
    pw[np.arange(R)[:, None], idx4[np.arange(R) % 512 // 64]] = h1
    pv = np.zeros((R, C))
    pv[np.arange(R)[:, None], idx5[np.arange(R) % 512 // 64]] = h1
    pu = np.zeros((R, C))
    pu[np.arange(R)[:, None], idx6[np.arange(R) % 512 // 64]] = h1
    g1 = np.maximum(pw + pv - pu, 0.0)
    hid = pick8(g1, idx7, 64) * f64(sb)
    hidq = mxq(hid, 0, "e4m3")
    y = wbu.T @ hidq
    return y

from contextlib import ExitStack

import concourse.mybir as mybir

K, J, R, T, Z, M, O, S, C, N = 512, 512, 512, 2048, 512, 1024, 256, 256, 512, 256
FLOPS = 2 * K * R * J + 2 * Z * R * J + 2 * R * N * O

F32 = mybir.dt.float32
BF16 = mybir.dt.bfloat16
I32 = mybir.dt.int32
U32 = mybir.dt.uint32
U16 = mybir.dt.uint16
U8 = mybir.dt.uint8
FP8X4 = mybir.dt.float8_e4m3fn_x4
FP4X4 = mybir.dt.float4_e2m1fn_x4
COPY = mybir.ActivationFunctionType.Copy
ALU = mybir.AluOpType

P = 128
PACK = 4
HALF_J = J // 2
HALF_O = O // 2


def load_scale_rows(queue, plane, rows):
    for q in range(4):
        queue.dma_start(plane[32 * q : 32 * q + 4, :].bitcast(I32), rows[0, 4 * q : 4 * q + 4, :].bitcast(I32))


def tile_picked_tokens_plain_bank_threeposts_one_plain_kernel(
    tc, xt_words, xt_scales, w_words, w_scales, xo_words, xo_scales, w2_words, w2_scales, sa, sb,
    wb_words, wb_scales, offs, offs2, offs3, offs4, offs5, offs6, offs7, out
):
    nc = tc.nc
    with ExitStack() as ctx:
        lists = ctx.enter_context(tc.tile_pool(name="lists", bufs=1))
        sbuf = ctx.enter_context(tc.tile_pool(name="sbuf", bufs=1))
        psum = ctx.enter_context(tc.psum_pool(name="psum", bufs=1))

        tok_list = lists.tile([P, J // 16], U16)
        note_list = lists.tile([P, J // 16], U16)
        slot_list = lists.tile([P, S // 16], U16)
        post_lists = [lists.tile([P, S // 16], U16, name="post_list%d" % i) for i in range(3)]
        place_list = lists.tile([P, O // 16], U16)

        xo_w = sbuf.tile([P, M], U16, align_bytes=64)
        xo_s = sbuf.tile([P, M], U8, align_bytes=64)
        xt_w = sbuf.tile([P, T], U16, align_bytes=64)
        xt_s = sbuf.tile([P, T], U8, align_bytes=64)
        w_raw = sbuf.tile([P, R], U32, align_bytes=64)
        w_raw_s = sbuf.tile([P, R], U8, align_bytes=64)
        w2_raw = sbuf.tile([P, R], U32, align_bytes=64)
        w2_raw_s = sbuf.tile([P, R], U8, align_bytes=64)
        wb_w = sbuf.tile([P, N], U32, align_bytes=64)
        wb_s = sbuf.tile([P, N], U8, align_bytes=64)
        sa_t = sbuf.tile([P, PACK], F32)
        sb_t = sbuf.tile([P, PACK], F32)

        for plane in (xo_s, xt_s, w2_raw_s, w_raw_s, wb_s):
            nc.vector.memset(plane[:].bitcast(I32), 0)
        boards = [[sbuf.tile([P, C], F32, name="board0_%d" % i, align_bytes=64) for i in range(3)]]
        for board in boards[0]:
            nc.vector.memset(board[:], 0.0)


        def words(src):
            return src[0].rearrange("p n t -> p (n t)").bitcast(I32)

        nc.sync.dma_start(xo_w[:].bitcast(I32), xo_words[0].bitcast(I32))
        nc.sync.dma_start(note_list[:], offs2)
        load_scale_rows(nc.scalar, xo_s, xo_scales)
        nc.sync.dma_start(xt_w[:].bitcast(I32), xt_words[0].bitcast(I32))
        nc.sync.dma_start(tok_list[:], offs)
        load_scale_rows(nc.sync, xt_s, xt_scales)
        nc.sync.dma_start(w2_raw[:].bitcast(I32), words(w2_words))
        nc.sync.dma_start(w_raw[:].bitcast(I32), words(w_words))
        load_scale_rows(nc.sync, w2_raw_s, w2_scales)
        load_scale_rows(nc.sync, w_raw_s, w_scales)
        nc.sync.dma_start(slot_list[:], offs3)
        nc.sync.dma_start(sa_t[:], sa.rearrange("(p t) o -> p (t o)", t=PACK))
        for post_list, src in zip(post_lists, (offs4, offs5, offs6)):
            nc.sync.dma_start(post_list[:], src)
        nc.sync.dma_start(place_list[:], offs7)
        nc.sync.dma_start(sb_t[:], sb.rearrange("(p t) o -> p (t o)", t=PACK))
        nc.sync.dma_start(wb_w[:].bitcast(I32), words(wb_words))
        load_scale_rows(nc.sync, wb_s, wb_scales)

        xo_gw = sbuf.tile([P, J], U16, align_bytes=64)
        xo_gs = sbuf.tile([P, J], U8, align_bytes=64)
        xt_gw = sbuf.tile([P, J], U16, align_bytes=64)
        xt_gs = sbuf.tile([P, J], U8, align_bytes=64)
        nc.vector.tensor_copy(xo_gw[:], xo_w[:].indirect(note_list[:]))
        nc.vector.tensor_copy(xo_gs[:], xo_s[:].indirect(note_list[:]))
        halves = [slice(h * HALF_J, (h + 1) * HALF_J) for h in range(2)]
        for cols in halves:
            entries = tok_list[:, cols.start // 16 : cols.stop // 16]
            nc.vector.tensor_copy(xt_gw[:, cols], xt_w[:].indirect(entries))
            nc.vector.tensor_copy(xt_gs[:, cols], xt_s[:].indirect(entries))

        w2_d = sbuf.tile([P, PACK, P], U32, tag="w2_dealt", align_bytes=64)
        w_d = sbuf.tile([P, PACK, P], U32, tag="w_dealt", align_bytes=64)
        for dealt, raw in ((w2_d, w2_raw), (w_d, w_raw)):
            nc.scalar.copy(dealt[:].rearrange("p t m -> p m t"), raw[:].rearrange("p (m t) -> p m t", t=PACK))
        w2_ds = [sbuf.tile([P, P], U8, name="w2_ds%d" % t, align_bytes=64) for t in range(PACK)]
        w_ds = [sbuf.tile([P, P], U8, name="w_ds%d" % t, align_bytes=64) for t in range(PACK)]
        for t in range(PACK):
            for dealt_s, raw_s in ((w2_ds, w2_raw_s), (w_ds, w_raw_s)):
                nc.gpsimd.tensor_copy(dealt_s[t][:], raw_s[:, t::PACK])

        def note_pass(acc, t, cols, start):
            nc.tensor.matmul_mx(out=acc, lhsT=w2_d[:, t, :].bitcast(FP8X4), lhsT_scale=w2_ds[t][:],
                                rhs=xo_gw[:, cols].bitcast(FP4X4), rhs_scale=xo_gs[:, cols],
                                start=start, stop=not start)

        def token_pass(acc, t, cols, start):
            nc.tensor.matmul_mx(out=acc, lhsT=w_d[:, t, :].bitcast(FP8X4), lhsT_scale=w_ds[t][:],
                                rhs=xt_gw[:, cols].bitcast(FP4X4), rhs_scale=xt_gs[:, cols],
                                start=start, stop=not start)

        a = [sbuf.tile([P, J], F32, name="a%d" % t, tag="a%d" % t, align_bytes=64) for t in range(PACK)]
        first = [psum.tile([P, HALF_J], F32, name="first%d" % h) for h in range(2)]
        for h in range(2):
            note_pass(first[h][:], 0, halves[h], True)
        for h in range(2):
            token_pass(first[h][:], 0, halves[h], False)
        nc.scalar.activation(a[0][:, halves[0]], first[0][:], COPY)
        nc.vector.tensor_copy(a[0][:, halves[1]], first[1][:])
        for t in range(1, PACK):
            acc = psum.tile([P, J], F32, name="acc%d" % t)
            token_pass(acc[:], t, slice(0, J), True)
            note_pass(acc[:], t, slice(0, J), False)
            nc.vector.tensor_copy(a[t][:], acc[:])

        h1 = [sbuf.tile([P, S], F32, name="h1_%d" % t) for t in range(PACK)]
        g1 = [sbuf.tile([P, C], F32, name="g1_%d" % t) for t in range(PACK)]

        def fetch_slots(t):
            nc.scalar.activation(h1[t][:], a[t][:].indirect(slot_list[:]), COPY, scale=sa_t[:, t : t + 1])

        def post(t, i):
            nc.scalar.activation(boards[t % 2][i][:].indirect(post_lists[i][:]), h1[t][:], COPY)

        fetch_slots(0)
        boards.append([sbuf.tile([P, C], F32, name="board1_%d" % i, tag=tag, align_bytes=64)
                       for i, tag in enumerate(("a0", "w_dealt", "w2_dealt"))])
        for board in boards[1]:
            nc.vector.memset(board[:], 0.0)
        for t in range(PACK):
            pw, pv, pu = boards[t % 2]
            post(t, 0)
            if t + 1 < PACK:
                fetch_slots(t + 1)
            post(t, 1)
            added = sbuf.tile([P, C], F32, name="added", bufs=2)
            nc.vector.tensor_tensor(added[:], pw[:], pv[:], ALU.add)
            post(t, 2)
            net = sbuf.tile([P, C], F32, name="net", bufs=2)
            nc.vector.tensor_tensor(net[:], added[:], pu[:], ALU.subtract)
            nc.vector.tensor_scalar_max(g1[t][:], net[:], 0.0)

        hid = sbuf.tile([P, PACK, O], BF16, align_bytes=64)
        for t in range(PACK - 1):
            nc.scalar.activation(hid[:, t, :], g1[t][:].indirect(place_list[:]), COPY, scale=sb_t[:, t : t + 1])
        place_halves = [slice(h * HALF_O, (h + 1) * HALF_O) for h in range(2)]
        last = PACK - 1
        for cols in place_halves:
            entries = place_list[:, cols.start // 16 : cols.stop // 16]
            nc.scalar.activation(hid[:, last, cols], g1[last][:].indirect(entries), COPY, scale=sb_t[:, last : last + 1])

        woven = [sbuf.tile([P, HALF_O, PACK], BF16, name="woven%d" % h, align_bytes=64) for h in range(2)]
        codes = [sbuf.tile([P, HALF_O], U32, name="codes%d" % h, align_bytes=64) for h in range(2)]
        hid_s = [sbuf.tile([P, HALF_O], U8, name="hid_s%d" % h, align_bytes=64) for h in range(2)]
        for h in range(2):
            nc.vector.tensor_copy(woven[h][:], hid[:, :, place_halves[h]].rearrange("p t o -> p o t"))
        for h in range(2):
            nc.vector.quantize_mx(out=codes[h][:].bitcast(FP8X4), scales=hid_s[h][:],
                                  in_=woven[h][:].rearrange("p o t -> p (o t)"))

        def out_pass(acc, u, h):
            rows = slice(u * P, (u + 1) * P)
            nc.tensor.matmul_mx(out=acc, lhsT=wb_w[:, rows].bitcast(FP8X4), lhsT_scale=wb_s[:, rows],
                                rhs=codes[h][:].bitcast(FP8X4), rhs_scale=hid_s[h][:], start=True, stop=True)

        y0 = psum.tile([P, 2, HALF_O], F32)
        for u in range(2):
            out_pass(y0[:, u, :], u, 0)
        y0_sb = sbuf.tile([P, 2, HALF_O], F32)
        nc.scalar.activation(y0_sb[:], y0[:], COPY)
        nc.sync.dma_start(out[:, place_halves[0]].rearrange("(u p) o -> p u o", p=P), y0_sb[:])
        y1 = [psum.tile([P, HALF_O], F32, name="y1_%d" % u) for u in range(2)]
        y1_sb = [sbuf.tile([P, HALF_O], F32, name="y1_sb%d" % u) for u in range(2)]
        for u in range(2):
            out_pass(y1[u][:], u, 1)
        nc.vector.tensor_copy(y1_sb[0][:], y1[0][:])
        nc.sync.dma_start(out[0:P, place_halves[1]], y1_sb[0][:])
        nc.scalar.activation(y1_sb[1][:], y1[1][:], COPY)
        nc.scalar.dma_start(out[P : 2 * P, place_halves[1]], y1_sb[1][:])
